import numpy as np, ml_dtypes
CORES = [71,199,95,223,103,231,111,239,119,247,127,255]
N = 12
WB, KB, QP = 1, 4, 64
def setup_inputs(rng):
    return {"q": rng.standard_normal((N, 128, QP), dtype=np.float32).astype(ml_dtypes.bfloat16), "k": rng.standard_normal((N, 128, KB * 128), dtype=np.float32).astype(ml_dtypes.bfloat16), "v": rng.standard_normal((N, 128, KB * 128), dtype=np.float32).astype(ml_dtypes.bfloat16)}
def setup_inputs_big(rng):
    d = setup_inputs(rng)
    for k in ("q", "k", "v"): d[k] = (d[k].astype(np.float32) * 1024.0).astype(d[k].dtype)
    return d
def setup_inputs_small(rng):
    d = setup_inputs(rng)
    for k in ("q", "k", "v"): d[k] = (d[k].astype(np.float32) * (1 / 1024.0)).astype(d[k].dtype)
    return d
def setup_inputs_apart(rng):
    d = setup_inputs(rng)
    f = (10.0 ** rng.permutation(np.linspace(-1.5, 1.5, N))).astype(np.float32).reshape(N, 1, 1)
    for k in ("q", "k", "v"): d[k] = (d[k].astype(np.float32) * f).astype(d[k].dtype)
    return d
def reference(q, k, v):
    Q, K, V = q.astype(np.float64), k.astype(np.float64), v.astype(np.float64)
    y = np.zeros((N, 128, QP))
    for r in range(N):
        for j in range(max(0, r - WB), r + 1):
            for b in range(KB):
                S = np.maximum(K[j][:, 128 * b:128 * b + 128].T @ Q[r], 0.0)
                y[r] += V[j][:, 128 * b:128 * b + 128].T @ S
    return {"y": y.astype(ml_dtypes.bfloat16 if q.dtype != np.float64 else np.float64)}

@@ -1,0 +1,145 @@
+from concourse.bass import DstId, RemoteDMATransfer
+from concourse.mybir import AluOpType
+
+KB, QP, BW = 4, 64, 128
+NE = 8
+
+SCRATCH = {
+    "qs": ("sbuf", [128, QP], "bfloat16"),
+    "ks": ("sbuf", [128, KB * BW], "bfloat16"),
+    "vs": ("sbuf", [128, KB * BW], "bfloat16"),
+    "qr": ("sbuf", [128, QP], "bfloat16"),
+    "orx": ("sbuf", [128, QP], "bfloat16"),
+    "kx": ("sbuf", [128, BW], "bfloat16"),
+    "vx": ("sbuf", [128, BW], "bfloat16"),
+    "zero": ("sbuf", [128, KB * QP], "bfloat16"),
+    "so": ("sbuf", [128, KB * QP], "bfloat16"),
+    "sr": ("sbuf", [128, KB * QP], "bfloat16"),
+    "sx": ("sbuf", [128, QP], "bfloat16"),
+    "osd": ("sbuf", [128, QP], "bfloat16"),
+    "ys": ("sbuf", [128, QP], "bfloat16"),
+    "pso": ("psum", [128, 512], "float32"),
+    "poo": ("psum", [128, 512], "float32"),
+    "por": ("psum", [128, 512], "float32"),
+    "ps0": ("psum", [128, 512], "float32"),
+    "ps1": ("psum", [128, 512], "float32"),
+    "ps2": ("psum", [128, 512], "float32"),
+    "ps3": ("psum", [128, 512], "float32"),
+}
+SEMAPHORES = ["qld", "kld", "vld", "xld", "qiss", "zs", "qarr", "oarr", "xarr", "lsem",
+              "om1", "orl", "om2", "xm1", "xrl", "m2", "cp", "yr", "yst"] \
+    + ["m1_%d" % b for b in range(KB)] + ["rl_%d" % b for b in range(KB)]
+
+
+def _engines(mask, n):
+    bits = [1 << i for i in range(16) if (mask >> i) & 1]
+    return bits[::len(bits) // n][:n]
+
+
+def rank_program(g, core, T, topo):
+    r = T.rank_of(core)
+    if r is None:
+        return
+    n = len(T.cores)
+    prev = T.cores[r - 1] if r > 0 else None
+    nxt = T.cores[r + 1] if r < n - 1 else None
+    ships = prev is None and nxt is not None
+    gets = r == 1
+    S = T.sem
+    te, ve, sy, sc = g.tensor, g.vector, g.sync, g.scalar
+
+    def blk(b):
+        return slice(b * BW, (b + 1) * BW)
+
+    def col(b):
+        return slice(b * QP, (b + 1) * QP)
+
+    ve.memset(T.zero[:], 0.0).then_inc(S.zs, 1)
+    if ships:
+        last, rest = blk(KB - 1), slice(0, (KB - 1) * BW)
+        sy.dma_start(T.ks[:, last], T.k[:, last]).then_inc(S.xld, 16)
+        sc.dma_start(T.vs[:, last], T.v[:, last]).then_inc(S.xld, 16)
+        sy.dma_start(T.qs[:], T.q[:]).then_inc(S.qld, 16)
+        sy.dma_start(T.ks[:, rest], T.k[:, rest]).then_inc(S.kld, 16)
+        sc.dma_start(T.vs[:, rest], T.v[:, rest]).then_inc(S.vld, 16)
+    else:
+        sy.dma_start(T.qs[:], T.q[:]).then_inc(S.qld, 16)
+        sy.sem_inc(S.qiss, 1)
+        sy.dma_start(T.ks[:], T.k[:]).then_inc(S.kld, 16)
+        sc.wait_ge(S.qiss, 1)
+        sc.dma_start(T.vs[:], T.v[:]).then_inc(S.vld, 16)
+
+    sent = 0
+    if prev is not None:
+        rid, pid = topo.addr(prev, core)
+        g.wait_ge(S.qld, 16)
+        g.remote_dma(out_ap=T.qr[:], in_ap=T.qs[:], remote_sem=S.qarr, local_sem=S.lsem, pid=pid, routing_id=rid,
+                     dma_engine_mask=sum(_engines(topo.mask(core, prev), NE)))
+        sent += NE
+    if ships:
+        rid, pid = topo.addr(nxt, core)
+        eng = _engines(topo.mask(core, nxt), NE)
+        g.wait_ge(S.xld, 32)
+        g.remote_dma_fused([
+            RemoteDMATransfer(dst_ids=[DstId(rid=rid, pnc=pid)], dma_engine_mask=sum(eng[:NE // 2]), remote_sem=S.xarr,
+                              src=T.ks[:, blk(KB - 1)], dst=T.kx[:]),
+            RemoteDMATransfer(dst_ids=[DstId(rid=rid, pnc=pid)], dma_engine_mask=sum(eng[NE // 2:]), remote_sem=S.xarr,
+                              src=T.vs[:, blk(KB - 1)], dst=T.vx[:]),
+        ], local_sem=S.lsem)
+        sent += NE
+
+    te.wait_ge(S.qld, 16)
+    te.wait_ge(S.kld, 16)
+    if ships:
+        te.wait_ge(S.xld, 32)
+    for b in range(KB):
+        te.matmul(out=T.pso[:, col(b)], lhsT=T.ks[:, blk(b)], rhs=T.qs[:], start=True, stop=True).then_inc(S.om1, 1)
+    ve.wait_ge(S.zs, 1)
+    ve.wait_ge(S.om1, KB)
+    ve.tensor_tensor(out=T.so[:], in0=T.pso[:, 0:KB * QP], in1=T.zero[:], op=AluOpType.max).then_inc(S.orl, 1)
+    te.wait_ge(S.orl, 1)
+    te.wait_ge(S.vld, 16)
+    for b in range(KB):
+        te.matmul(out=T.poo[:, 0:QP], lhsT=T.vs[:, blk(b)], rhs=T.so[:, col(b)], start=(b == 0),
+                  stop=(b == KB - 1 and not gets)).then_inc(S.om2, 1)
+
+    if nxt is not None:
+        nb = KB - 1 if ships else KB
+        te.wait_ge(S.qarr, NE)
+        for b in range(nb):
+            te.matmul(out=T["ps%d" % b][:, 0:QP], lhsT=T.ks[:, blk(b)], rhs=T.qr[:], start=True,
+                      stop=True).then_inc(S["m1_%d" % b], 1)
+        for b in range(nb):
+            ve.wait_ge(S["m1_%d" % b], 1)
+            ve.tensor_tensor(out=T.sr[:, col(b)], in0=T["ps%d" % b][:, 0:QP], in1=T.zero[:, 0:QP],
+                             op=AluOpType.max).then_inc(S["rl_%d" % b], 1)
+            te.wait_ge(S["rl_%d" % b], 1)
+            te.matmul(out=T.por[:, 0:QP], lhsT=T.vs[:, blk(b)], rhs=T.sr[:, col(b)], start=(b == 0),
+                      stop=(b == nb - 1)).then_inc(S.m2, 1)
+        ve.wait_ge(S.m2, nb)
+        ve.tensor_copy(out=T.osd[:], in_=T.por[:, 0:QP]).then_inc(S.cp, 1)
+        rid, pid = topo.addr(nxt, core)
+        g.wait_ge(S.cp, 1)
+        g.remote_dma(out_ap=T.orx[:], in_ap=T.osd[:], remote_sem=S.oarr, local_sem=S.lsem, pid=pid, routing_id=rid,
+                     dma_engine_mask=sum(_engines(topo.mask(core, nxt), NE)))
+        sent += NE
+
+    if gets:
+        te.wait_ge(S.xarr, NE)
+        te.matmul(out=T.pso[:, 0:QP], lhsT=T.kx[:], rhs=T.qs[:], start=True, stop=True).then_inc(S.xm1, 1)
+        ve.wait_ge(S.xm1, 1)
+        ve.tensor_tensor(out=T.sx[:], in0=T.pso[:, 0:QP], in1=T.zero[:, 0:QP], op=AluOpType.max).then_inc(S.xrl, 1)
+        te.wait_ge(S.xrl, 1)
+        te.matmul(out=T.poo[:, 0:QP], lhsT=T.vx[:], rhs=T.sx[:], start=False, stop=True).then_inc(S.om2, 1)
+
+    ve.wait_ge(S.om2, KB + (1 if gets else 0))
+    if prev is not None:
+        ve.wait_ge(S.oarr, NE)
+        ve.tensor_tensor(out=T.ys[:], in0=T.poo[:, 0:QP], in1=T.orx[:], op=AluOpType.add).then_inc(S.yr, 1)
+    else:
+        ve.tensor_copy(out=T.ys[:], in_=T.poo[:, 0:QP]).then_inc(S.yr, 1)
+    sy.wait_ge(S.yr, 1)
+    sy.dma_start(T.y[:], T.ys[:]).then_inc(S.yst, 16)
+    sy.wait_ge(S.yst, 16)
+    if sent:
+        g.wait_ge(S.lsem, sent)

@@ -3,22 +3,28 @@ from concourse.mybir import AluOpType
 
 KB, QP, BW = 4, 64, 128
 NE = 8
+HB = KB // 2
 
 SCRATCH = {
+    "qd": ("dram", [128, QP], "bfloat16"),
+    "yl": ("dram", [128, QP], "bfloat16"),
     "qs": ("sbuf", [128, QP], "bfloat16"),
     "ks": ("sbuf", [128, KB * BW], "bfloat16"),
     "vs": ("sbuf", [128, KB * BW], "bfloat16"),
     "qr": ("sbuf", [128, QP], "bfloat16"),
+    "prx": ("sbuf", [128, QP], "bfloat16"),
     "orx": ("sbuf", [128, QP], "bfloat16"),
     "kx": ("sbuf", [128, BW], "bfloat16"),
     "vx": ("sbuf", [128, BW], "bfloat16"),
-    "zero": ("sbuf", [128, KB * QP], "bfloat16"),
+    "zero": ("sbuf", [128, HB * QP], "bfloat16"),
     "so": ("sbuf", [128, KB * QP], "bfloat16"),
     "sr": ("sbuf", [128, KB * QP], "bfloat16"),
     "sx": ("sbuf", [128, QP], "bfloat16"),
+    "psd": ("sbuf", [128, QP], "bfloat16"),
     "osd": ("sbuf", [128, QP], "bfloat16"),
     "ys": ("sbuf", [128, QP], "bfloat16"),
-    "pso": ("psum", [128, 512], "float32"),
+    "pa0": ("psum", [128, 512], "float32"),
+    "pa1": ("psum", [128, 512], "float32"),
     "poo": ("psum", [128, 512], "float32"),
     "por": ("psum", [128, 512], "float32"),
     "ps0": ("psum", [128, 512], "float32"),
@@ -26,8 +32,8 @@ SCRATCH = {
     "ps2": ("psum", [128, 512], "float32"),
     "ps3": ("psum", [128, 512], "float32"),
 }
-SEMAPHORES = ["qld", "kld", "vld", "xld", "qiss", "zs", "qarr", "oarr", "xarr", "lsem",
-              "om1", "orl", "om2", "xm1", "xrl", "m2", "cp", "yr", "yst"] \
+SEMAPHORES = ["qdl", "qld", "kld", "vld", "xld", "qiss", "kiss", "zs", "qarr", "parr", "oarr", "yarr", "xarr", "lsem",
+              "om1_0", "om1_1", "orl_0", "orl_1", "om2", "pcp", "xm1", "xrl", "m2", "cp", "yr", "yst"] \
     + ["m1_%d" % b for b in range(KB)] + ["rl_%d" % b for b in range(KB)]
 
 
@@ -45,8 +51,10 @@ def rank_program(g, core, T, topo):
     nxt = T.cores[r + 1] if r < n - 1 else None
     ships = prev is None and nxt is not None
     gets = r == 1
+    sends_p = prev is not None and not gets
     S = T.sem
     te, ve, sy, sc = g.tensor, g.vector, g.sync, g.scalar
+    sent = [0]
 
     def blk(b):
         return slice(b * BW, (b + 1) * BW)
@@ -54,28 +62,34 @@ def rank_program(g, core, T, topo):
     def col(b):
         return slice(b * QP, (b + 1) * QP)
 
+    def write(dst_core, out_ap, in_ap, sem):
+        rid, pid = topo.addr(dst_core, core)
+        g.remote_dma(out_ap=out_ap, in_ap=in_ap, remote_sem=sem, local_sem=S.lsem, pid=pid, routing_id=rid,
+                     dma_engine_mask=sum(_engines(topo.mask(core, dst_core), NE)))
+        sent[0] += NE
+
     ve.memset(T.zero[:], 0.0).then_inc(S.zs, 1)
+    ve.wait_ge(S.zs, 1)
     if ships:
         last, rest = blk(KB - 1), slice(0, (KB - 1) * BW)
         sy.dma_start(T.ks[:, last], T.k[:, last]).then_inc(S.xld, 16)
         sc.dma_start(T.vs[:, last], T.v[:, last]).then_inc(S.xld, 16)
-        sy.dma_start(T.qs[:], T.q[:]).then_inc(S.qld, 16)
         sy.dma_start(T.ks[:, rest], T.k[:, rest]).then_inc(S.kld, 16)
         sc.dma_start(T.vs[:, rest], T.v[:, rest]).then_inc(S.vld, 16)
-    else:
         sy.dma_start(T.qs[:], T.q[:]).then_inc(S.qld, 16)
+    else:
+        sy.dma_start(T.qd[:], T.q[:]).then_inc(S.qdl, 16)
         sy.sem_inc(S.qiss, 1)
         sy.dma_start(T.ks[:], T.k[:]).then_inc(S.kld, 16)
+        sy.sem_inc(S.kiss, 1)
         sc.wait_ge(S.qiss, 1)
+        sc.dma_start(T.qs[:], T.q[:]).then_inc(S.qld, 16)
+        sc.wait_ge(S.kiss, 1)
         sc.dma_start(T.vs[:], T.v[:]).then_inc(S.vld, 16)
 
-    sent = 0
     if prev is not None:
-        rid, pid = topo.addr(prev, core)
-        g.wait_ge(S.qld, 16)
-        g.remote_dma(out_ap=T.qr[:], in_ap=T.qs[:], remote_sem=S.qarr, local_sem=S.lsem, pid=pid, routing_id=rid,
-                     dma_engine_mask=sum(_engines(topo.mask(core, prev), NE)))
-        sent += NE
+        g.wait_ge(S.qdl, 16)
+        write(prev, T.qr[:], T.qd[:], S.qarr)
     if ships:
         rid, pid = topo.addr(nxt, core)
         eng = _engines(topo.mask(core, nxt), NE)
@@ -86,29 +100,43 @@ def rank_program(g, core, T, topo):
             RemoteDMATransfer(dst_ids=[DstId(rid=rid, pnc=pid)], dma_engine_mask=sum(eng[NE // 2:]), remote_sem=S.xarr,
                               src=T.vs[:, blk(KB - 1)], dst=T.vx[:]),
         ], local_sem=S.lsem)
-        sent += NE
+        sent[0] += NE
 
-    te.wait_ge(S.qld, 16)
-    te.wait_ge(S.kld, 16)
-    if ships:
-        te.wait_ge(S.xld, 32)
-    for b in range(KB):
-        te.matmul(out=T.pso[:, col(b)], lhsT=T.ks[:, blk(b)], rhs=T.qs[:], start=True, stop=True).then_inc(S.om1, 1)
-    ve.wait_ge(S.zs, 1)
-    ve.wait_ge(S.om1, KB)
-    ve.tensor_tensor(out=T.so[:], in0=T.pso[:, 0:KB * QP], in1=T.zero[:], op=AluOpType.max).then_inc(S.orl, 1)
-    te.wait_ge(S.orl, 1)
-    te.wait_ge(S.vld, 16)
-    for b in range(KB):
-        te.matmul(out=T.poo[:, 0:QP], lhsT=T.vs[:, blk(b)], rhs=T.so[:, col(b)], start=(b == 0),
-                  stop=(b == KB - 1 and not gets)).then_inc(S.om2, 1)
+    def own():
+        te.wait_ge(S.qld, 16)
+        te.wait_ge(S.kld, 16)
+        if ships:
+            te.wait_ge(S.xld, 32)
+        for h in range(2):
+            for i in range(HB):
+                te.matmul(out=T["pa%d" % h][:, col(i)], lhsT=T.ks[:, blk(h * HB + i)], rhs=T.qs[:], start=True,
+                          stop=True).then_inc(S["om1_%d" % h], 1)
+        for h in range(2):
+            ve.wait_ge(S["om1_%d" % h], HB)
+            ve.tensor_tensor(out=T.so[:, h * HB * QP:(h + 1) * HB * QP], in0=T["pa%d" % h][:, 0:HB * QP], in1=T.zero[:],
+                             op=AluOpType.max).then_inc(S["orl_%d" % h], 1)
+        te.wait_ge(S.vld, 16)
+        for h in range(2):
+            te.wait_ge(S["orl_%d" % h], 1)
+            for b in range(h * HB, (h + 1) * HB):
+                te.matmul(out=T.poo[:, 0:QP], lhsT=T.vs[:, blk(b)], rhs=T.so[:, col(b)], start=(b == 0),
+                          stop=(b == KB - 1 and not gets)).then_inc(S.om2, 1)
+        if sends_p:
+            ve.wait_ge(S.om2, KB)
+            ve.tensor_copy(out=T.psd[:], in_=T.poo[:, 0:QP]).then_inc(S.pcp, 1)
+            g.wait_ge(S.pcp, 1)
+            write(prev, T.prx[:], T.psd[:], S.parr)
 
-    if nxt is not None:
+    def neighbour():
         nb = KB - 1 if ships else KB
+        if ships:
+            te.wait_ge(S.kld, 16)
         te.wait_ge(S.qarr, NE)
         for b in range(nb):
             te.matmul(out=T["ps%d" % b][:, 0:QP], lhsT=T.ks[:, blk(b)], rhs=T.qr[:], start=True,
                       stop=True).then_inc(S["m1_%d" % b], 1)
+        if ships:
+            te.wait_ge(S.vld, 16)
         for b in range(nb):
             ve.wait_ge(S["m1_%d" % b], 1)
             ve.tensor_tensor(out=T.sr[:, col(b)], in0=T["ps%d" % b][:, 0:QP], in1=T.zero[:, 0:QP],
@@ -117,29 +145,44 @@ def rank_program(g, core, T, topo):
             te.matmul(out=T.por[:, 0:QP], lhsT=T.vs[:, blk(b)], rhs=T.sr[:, col(b)], start=(b == 0),
                       stop=(b == nb - 1)).then_inc(S.m2, 1)
         ve.wait_ge(S.m2, nb)
-        ve.tensor_copy(out=T.osd[:], in_=T.por[:, 0:QP]).then_inc(S.cp, 1)
-        rid, pid = topo.addr(nxt, core)
-        g.wait_ge(S.cp, 1)
-        g.remote_dma(out_ap=T.orx[:], in_ap=T.osd[:], remote_sem=S.oarr, local_sem=S.lsem, pid=pid, routing_id=rid,
-                     dma_engine_mask=sum(_engines(topo.mask(core, nxt), NE)))
-        sent += NE
+        if ships:
+            ve.tensor_copy(out=T.osd[:], in_=T.por[:, 0:QP]).then_inc(S.cp, 1)
+            g.wait_ge(S.cp, 1)
+            write(nxt, T.orx[:], T.osd[:], S.oarr)
+        else:
+            ve.wait_ge(S.parr, NE)
+            ve.tensor_tensor(out=T.osd[:], in0=T.por[:, 0:QP], in1=T.prx[:], op=AluOpType.add).then_inc(S.cp, 1)
+            g.wait_ge(S.cp, 1)
+            write(nxt, T.yl[:], T.osd[:], S.yarr)
+
+    if ships:
+        neighbour()
+        own()
+    else:
+        own()
+        if nxt is not None:
+            neighbour()
 
     if gets:
         te.wait_ge(S.xarr, NE)
-        te.matmul(out=T.pso[:, 0:QP], lhsT=T.kx[:], rhs=T.qs[:], start=True, stop=True).then_inc(S.xm1, 1)
+        te.matmul(out=T.pa0[:, 0:QP], lhsT=T.kx[:], rhs=T.qs[:], start=True, stop=True).then_inc(S.xm1, 1)
         ve.wait_ge(S.xm1, 1)
-        ve.tensor_tensor(out=T.sx[:], in0=T.pso[:, 0:QP], in1=T.zero[:, 0:QP], op=AluOpType.max).then_inc(S.xrl, 1)
+        ve.tensor_tensor(out=T.sx[:], in0=T.pa0[:, 0:QP], in1=T.zero[:, 0:QP], op=AluOpType.max).then_inc(S.xrl, 1)
         te.wait_ge(S.xrl, 1)
         te.matmul(out=T.poo[:, 0:QP], lhsT=T.vx[:], rhs=T.sx[:], start=False, stop=True).then_inc(S.om2, 1)
 
-    ve.wait_ge(S.om2, KB + (1 if gets else 0))
-    if prev is not None:
-        ve.wait_ge(S.oarr, NE)
-        ve.tensor_tensor(out=T.ys[:], in0=T.poo[:, 0:QP], in1=T.orx[:], op=AluOpType.add).then_inc(S.yr, 1)
+    if sends_p:
+        sy.wait_ge(S.yarr, NE)
+        sy.dma_start(T.y[:], T.yl[:]).then_inc(S.yst, 16)
     else:
-        ve.tensor_copy(out=T.ys[:], in_=T.poo[:, 0:QP]).then_inc(S.yr, 1)
-    sy.wait_ge(S.yr, 1)
-    sy.dma_start(T.y[:], T.ys[:]).then_inc(S.yst, 16)
+        ve.wait_ge(S.om2, KB + (1 if gets else 0))
+        if gets:
+            ve.wait_ge(S.oarr, NE)
+            ve.tensor_tensor(out=T.ys[:], in0=T.poo[:, 0:QP], in1=T.orx[:], op=AluOpType.add).then_inc(S.yr, 1)
+        else:
+            ve.tensor_copy(out=T.ys[:], in_=T.poo[:, 0:QP]).then_inc(S.yr, 1)
+        sy.wait_ge(S.yr, 1)
+        sy.dma_start(T.y[:], T.ys[:]).then_inc(S.yst, 16)
     sy.wait_ge(S.yst, 16)
-    if sent:
-        g.wait_ge(S.lsem, sent)
+    if sent[0]:
+        g.wait_ge(S.lsem, sent[0])

from concourse.bass import DstId, RemoteDMATransfer
from concourse.mybir import AluOpType

KB, QP, BW = 4, 64, 128
NE = 8
HB = KB // 2

SCRATCH = {
    "qd": ("dram", [128, QP], "bfloat16"),
    "yl": ("dram", [128, QP], "bfloat16"),
    "qs": ("sbuf", [128, QP], "bfloat16"),
    "ks": ("sbuf", [128, KB * BW], "bfloat16"),
    "vs": ("sbuf", [128, KB * BW], "bfloat16"),
    "qr": ("sbuf", [128, QP], "bfloat16"),
    "prx": ("sbuf", [128, QP], "bfloat16"),
    "orx": ("sbuf", [128, QP], "bfloat16"),
    "kx": ("sbuf", [128, BW], "bfloat16"),
    "vx": ("sbuf", [128, BW], "bfloat16"),
    "zero": ("sbuf", [128, HB * QP], "bfloat16"),
    "so": ("sbuf", [128, KB * QP], "bfloat16"),
    "sr": ("sbuf", [128, KB * QP], "bfloat16"),
    "sx": ("sbuf", [128, QP], "bfloat16"),
    "psd": ("sbuf", [128, QP], "bfloat16"),
    "osd": ("sbuf", [128, QP], "bfloat16"),
    "ys": ("sbuf", [128, QP], "bfloat16"),
    "pa0": ("psum", [128, 512], "float32"),
    "pa1": ("psum", [128, 512], "float32"),
    "poo": ("psum", [128, 512], "float32"),
    "por": ("psum", [128, 512], "float32"),
    "ps0": ("psum", [128, 512], "float32"),
    "ps1": ("psum", [128, 512], "float32"),
    "ps2": ("psum", [128, 512], "float32"),
    "ps3": ("psum", [128, 512], "float32"),
}
SEMAPHORES = ["qdl", "qld", "kld", "vld", "xld", "qiss", "kiss", "zs", "qarr", "parr", "oarr", "yarr", "xarr", "lsem",
              "om1_0", "om1_1", "orl_0", "orl_1", "om2", "pcp", "xm1", "xrl", "m2", "cp", "yr", "yst"] \
    + ["m1_%d" % b for b in range(KB)] + ["rl_%d" % b for b in range(KB)]


def _engines(mask, n):
    bits = [1 << i for i in range(16) if (mask >> i) & 1]
    return bits[::len(bits) // n][:n]


def rank_program(g, core, T, topo):
    r = T.rank_of(core)
    if r is None:
        return
    n = len(T.cores)
    prev = T.cores[r - 1] if r > 0 else None
    nxt = T.cores[r + 1] if r < n - 1 else None
    ships = prev is None and nxt is not None
    gets = r == 1
    sends_p = prev is not None and not gets
    S = T.sem
    te, ve, sy, sc = g.tensor, g.vector, g.sync, g.scalar
    sent = [0]

    def blk(b):
        return slice(b * BW, (b + 1) * BW)

    def col(b):
        return slice(b * QP, (b + 1) * QP)

    def write(dst_core, out_ap, in_ap, sem):
        rid, pid = topo.addr(dst_core, core)
        g.remote_dma(out_ap=out_ap, in_ap=in_ap, remote_sem=sem, local_sem=S.lsem, pid=pid, routing_id=rid,
                     dma_engine_mask=sum(_engines(topo.mask(core, dst_core), NE)))
        sent[0] += NE

    ve.memset(T.zero[:], 0.0).then_inc(S.zs, 1)
    ve.wait_ge(S.zs, 1)
    if ships:
        last, rest = blk(KB - 1), slice(0, (KB - 1) * BW)
        sy.dma_start(T.ks[:, last], T.k[:, last]).then_inc(S.xld, 16)
        sc.dma_start(T.vs[:, last], T.v[:, last]).then_inc(S.xld, 16)
        sy.dma_start(T.ks[:, rest], T.k[:, rest]).then_inc(S.kld, 16)
        sc.dma_start(T.vs[:, rest], T.v[:, rest]).then_inc(S.vld, 16)
        sy.dma_start(T.qs[:], T.q[:]).then_inc(S.qld, 16)
    else:
        sy.dma_start(T.qd[:], T.q[:]).then_inc(S.qdl, 16)
        sy.sem_inc(S.qiss, 1)
        sy.dma_start(T.ks[:], T.k[:]).then_inc(S.kld, 16)
        sy.sem_inc(S.kiss, 1)
        sc.wait_ge(S.qiss, 1)
        sc.dma_start(T.qs[:], T.q[:]).then_inc(S.qld, 16)
        sc.wait_ge(S.kiss, 1)
        sc.dma_start(T.vs[:], T.v[:]).then_inc(S.vld, 16)

    if prev is not None:
        g.wait_ge(S.qdl, 16)
        write(prev, T.qr[:], T.qd[:], S.qarr)
    if ships:
        rid, pid = topo.addr(nxt, core)
        eng = _engines(topo.mask(core, nxt), NE)
        g.wait_ge(S.xld, 32)
        g.remote_dma_fused([
            RemoteDMATransfer(dst_ids=[DstId(rid=rid, pnc=pid)], dma_engine_mask=sum(eng[:NE // 2]), remote_sem=S.xarr,
                              src=T.ks[:, blk(KB - 1)], dst=T.kx[:]),
            RemoteDMATransfer(dst_ids=[DstId(rid=rid, pnc=pid)], dma_engine_mask=sum(eng[NE // 2:]), remote_sem=S.xarr,
                              src=T.vs[:, blk(KB - 1)], dst=T.vx[:]),
        ], local_sem=S.lsem)
        sent[0] += NE

    def own():
        te.wait_ge(S.qld, 16)
        te.wait_ge(S.kld, 16)
        if ships:
            te.wait_ge(S.xld, 32)
        for h in range(2):
            for i in range(HB):
                te.matmul(out=T["pa%d" % h][:, col(i)], lhsT=T.ks[:, blk(h * HB + i)], rhs=T.qs[:], start=True,
                          stop=True).then_inc(S["om1_%d" % h], 1)
        for h in range(2):
            ve.wait_ge(S["om1_%d" % h], HB)
            ve.tensor_tensor(out=T.so[:, h * HB * QP:(h + 1) * HB * QP], in0=T["pa%d" % h][:, 0:HB * QP], in1=T.zero[:],
                             op=AluOpType.max).then_inc(S["orl_%d" % h], 1)
        te.wait_ge(S.vld, 16)
        for h in range(2):
            te.wait_ge(S["orl_%d" % h], 1)
            for b in range(h * HB, (h + 1) * HB):
                te.matmul(out=T.poo[:, 0:QP], lhsT=T.vs[:, blk(b)], rhs=T.so[:, col(b)], start=(b == 0),
                          stop=(b == KB - 1 and not gets)).then_inc(S.om2, 1)
        if sends_p:
            ve.wait_ge(S.om2, KB)
            ve.tensor_copy(out=T.psd[:], in_=T.poo[:, 0:QP]).then_inc(S.pcp, 1)
            g.wait_ge(S.pcp, 1)
            write(prev, T.prx[:], T.psd[:], S.parr)

    def neighbour():
        nb = KB - 1 if ships else KB
        if ships:
            te.wait_ge(S.kld, 16)
        te.wait_ge(S.qarr, NE)
        for b in range(nb):
            te.matmul(out=T["ps%d" % b][:, 0:QP], lhsT=T.ks[:, blk(b)], rhs=T.qr[:], start=True,
                      stop=True).then_inc(S["m1_%d" % b], 1)
        if ships:
            te.wait_ge(S.vld, 16)
        for b in range(nb):
            ve.wait_ge(S["m1_%d" % b], 1)
            ve.tensor_tensor(out=T.sr[:, col(b)], in0=T["ps%d" % b][:, 0:QP], in1=T.zero[:, 0:QP],
                             op=AluOpType.max).then_inc(S["rl_%d" % b], 1)
            te.wait_ge(S["rl_%d" % b], 1)
            te.matmul(out=T.por[:, 0:QP], lhsT=T.vs[:, blk(b)], rhs=T.sr[:, col(b)], start=(b == 0),
                      stop=(b == nb - 1)).then_inc(S.m2, 1)
        ve.wait_ge(S.m2, nb)
        if ships:
            ve.tensor_copy(out=T.osd[:], in_=T.por[:, 0:QP]).then_inc(S.cp, 1)
            g.wait_ge(S.cp, 1)
            write(nxt, T.orx[:], T.osd[:], S.oarr)
        else:
            ve.wait_ge(S.parr, NE)
            ve.tensor_tensor(out=T.osd[:], in0=T.por[:, 0:QP], in1=T.prx[:], op=AluOpType.add).then_inc(S.cp, 1)
            g.wait_ge(S.cp, 1)
            write(nxt, T.yl[:], T.osd[:], S.yarr)

    if ships:
        neighbour()
        own()
    else:
        own()
        if nxt is not None:
            neighbour()

    if gets:
        te.wait_ge(S.xarr, NE)
        te.matmul(out=T.pa0[:, 0:QP], lhsT=T.kx[:], rhs=T.qs[:], start=True, stop=True).then_inc(S.xm1, 1)
        ve.wait_ge(S.xm1, 1)
        ve.tensor_tensor(out=T.sx[:], in0=T.pa0[:, 0:QP], in1=T.zero[:, 0:QP], op=AluOpType.max).then_inc(S.xrl, 1)
        te.wait_ge(S.xrl, 1)
        te.matmul(out=T.poo[:, 0:QP], lhsT=T.vx[:], rhs=T.sx[:], start=False, stop=True).then_inc(S.om2, 1)

    if sends_p:
        sy.wait_ge(S.yarr, NE)
        sy.dma_start(T.y[:], T.yl[:]).then_inc(S.yst, 16)
    else:
        ve.wait_ge(S.om2, KB + (1 if gets else 0))
        if gets:
            ve.wait_ge(S.oarr, NE)
            ve.tensor_tensor(out=T.ys[:], in0=T.poo[:, 0:QP], in1=T.orx[:], op=AluOpType.add).then_inc(S.yr, 1)
        else:
            ve.tensor_copy(out=T.ys[:], in_=T.poo[:, 0:QP]).then_inc(S.yr, 1)
        sy.wait_ge(S.yr, 1)
        sy.dma_start(T.y[:], T.ys[:]).then_inc(S.yst, 16)
    sy.wait_ge(S.yst, 16)
    if sent[0]:
        g.wait_ge(S.lsem, sent[0])
